import numpy as np, ml_dtypes
CORES = [65,73,81,89,97,105,113,121]
N = 8
QP = 128
def setup_inputs(rng):
    m = 150 * rng.standard_normal((1, QP, 1), dtype=np.float32) + 3 * rng.standard_normal((N, QP, 1), dtype=np.float32)
    m = (m + rng.uniform(100, 300, (1, QP, 1)) * (rng.random((1, QP, 1)) < 0.7) * (rng.random((N, QP, 1)) < 0.5)).astype(np.float32)
    l = 20 * (1 + np.abs(rng.standard_normal((N, QP, 1), dtype=np.float32)))
    return {"o": (l * rng.standard_normal((N, QP, 128), dtype=np.float32) / 4).astype(ml_dtypes.bfloat16), "ml": np.concatenate([m, l], axis=2)}
def setup_inputs_big(rng):
    d = setup_inputs(rng)
    for k in ("o",): d[k] = (d[k].astype(np.float32) * 1048576.0).astype(d[k].dtype)
    return d
def setup_inputs_small(rng):
    d = setup_inputs(rng)
    for k in ("o",): d[k] = (d[k].astype(np.float32) * (1 / 1048576.0)).astype(d[k].dtype)
    return d
def setup_inputs_apart(rng):
    d = setup_inputs(rng)
    f = (10.0 ** rng.permutation(np.linspace(-1.5, 1.5, N))).astype(np.float32).reshape(N, 1, 1)
    for k in ("o",): d[k] = (d[k].astype(np.float32) * f).astype(d[k].dtype)
    return d
def reference(o, ml):
    O, ML = o.astype(np.float64), ml.astype(np.float64)
    m, l = ML[:, :, 0:1], ML[:, :, 1:2]
    f = np.exp(m - m.max(axis=0))
    y = ((f * O).sum(axis=0) / (f * l).sum(axis=0)).astype(ml_dtypes.bfloat16)
    return {"y": np.stack([y[QP // N * r:QP // N * (r + 1)] for r in range(N)])}

@@ -1,0 +1,169 @@
+from concourse.bass import DstId, RemoteDMATransfer
+from concourse.mybir import AluOpType, AxisListType, ActivationFunctionType
+
+SCRATCH = {
+    "opc": ("dram", [8, 128, 16], "bfloat16"),
+    "mls": ("dram", [128, 2], "float32"),
+    "og": ("dram", [7, 128, 16], "bfloat16"),
+    "mlg": ("dram", [7, 128, 2], "float32"),
+    "O": ("sbuf", [128, 136], "bfloat16"),
+    "A": ("sbuf", [128, 2], "float32"),
+    "zz": ("sbuf", [128, 128], "bfloat16"),
+    "ones": ("sbuf", [128, 128], "bfloat16"),
+    "P": ("sbuf", [128, 128], "bfloat16"),
+    "X": ("sbuf", [128, 128], "bfloat16"),
+    "mj0": ("sbuf", [128, 8], "bfloat16"),
+    "MJ": ("sbuf", [128, 8], "bfloat16"),
+    "Y": ("sbuf", [128, 8], "bfloat16"),
+    "negM": ("sbuf", [128, 1], "float32"),
+    "f": ("sbuf", [128, 1], "float32"),
+    "W": ("sbuf", [128, 16], "bfloat16"),
+    "rec": ("sbuf", [128, 1], "float32"),
+    "yb": ("sbuf", [128, 128], "bfloat16"),
+    "PX": ("psum", [128, 512], "float32"),
+    "PM": ("psum", [128, 512], "float32"),
+    "PO": ("psum", [128, 512], "float32"),
+}
+SEMAPHORES = ["l1o", "l1ml", "sent", "mld", "od", "mlr", "orl", "sA", "sO", "sz", "sones", "sP", "sPX", "sX",
+              "smj0", "sMJ", "sY", "sL", "sPM", "snegM", "sf", "sW", "sPO", "srec", "syb", "done"]
+
+
+def _bits(mask):
+    return [1 << i for i in range(16) if (mask >> i) & 1]
+
+
+def _plan(T, topo):
+    cores = list(T.cores)
+    n = len(cores)
+    direct, relay, helper = [], [], []
+    for j in range(n):
+        c = cores[j]
+        direct.append([d for d in range(n) if d != j and topo.may_write(c, cores[d])])
+        relay.append([d for d in range(n) if d != j and not topo.may_write(c, cores[d])])
+        cand = [h for h in range(128)
+                if topo.chip(h) == topo.chip(c) and h not in cores
+                and all(topo.may_write(h, cores[d]) for d in relay[j])]
+        near = [h for h in cand if topo.die(h) == topo.die(c)]
+        helper.append((near or cand)[0])
+    return cores, direct, relay, helper
+
+
+def _slot(direct, relay, d, j):
+    n = len(direct)
+    order = [s for s in range(n) if d in direct[s]] + [s for s in range(n) if d in relay[s]]
+    return order.index(j)
+
+
+def _dst(topo, c):
+    rid, pid, _ = topo.addr(c)
+    return DstId(rid=rid, pnc=pid)
+
+
+def _engines(topo, src, dsts):
+    m = topo.mask(src, dsts[0])
+    for d in dsts[1:]:
+        m &= topo.mask(src, d)
+    e = _bits(m)
+    return e[0::2] + e[1::2]
+
+
+def _helper_program(g, core, T, topo, j, cores, direct, relay):
+    S = T.sem
+    ds = relay[j]
+    eng = _engines(topo, core, [cores[d] for d in ds])
+    g.wait_ge(S.mld, 1)
+    g.remote_dma_fused([RemoteDMATransfer(
+        dst_ids=[_dst(topo, cores[d]) for d in ds], dma_engine_mask=eng[0], remote_sem=S.mlr,
+        srcs=[T.mls[:, :]], dsts=[T.mlg[_slot(direct, relay, d, j)] for d in ds])], local_sem=S.sent)
+    g.wait_ge(S.od, len(ds))
+    g.remote_dma_fused([RemoteDMATransfer(
+        dst_ids=[_dst(topo, cores[d])], dma_engine_mask=eng[i], remote_sem=S.orl,
+        src=T.opc[d], dst=T.og[_slot(direct, relay, d, j)]) for i, d in enumerate(ds)], local_sem=S.sent)
+    g.wait_ge(S.sent, 1 + len(ds))
+
+
+def rank_program(g, core, T, topo):
+    cores, direct, relay, helper = _plan(T, topo)
+    r = T.rank_of(core)
+    if r is None:
+        if core in helper:
+            _helper_program(g, core, T, topo, helper.index(core), cores, direct, relay)
+        return
+    S = T.sem
+    mult = AluOpType.mult
+    Exp = ActivationFunctionType.Exp
+    nd = len([s for s in range(len(cores)) if r in direct[s]])
+    nr = len([s for s in range(len(cores)) if r in relay[s]])
+    q0, pd, pr = 16 * r, 16 * nd, 16 * (nd + nr)
+    hc = helper[r]
+
+    g.sync.dma_start(T.opc[:], T.o[:, :]).then_inc(S.l1o, 16)
+    g.scalar.dma_start(T.mls[:, :], T.ml[:, :]).then_inc(S.l1ml, 16)
+    g.sync.dma_start(T.O[pr:128, 0:128], T.o[q0:q0 + 16, :]).then_inc(S.sO, 16)
+    g.scalar.dma_start(T.A[pr:128, :], T.ml[q0:q0 + 16, :]).then_inc(S.sA, 16)
+
+    g.vector.memset(T.zz[:, :], 0.0).then_inc(S.sz, 1)
+    g.scalar.wait_ge(S.sz, 1)
+    g.scalar.activation(T.ones[:, :], T.zz[:, :], Exp).then_inc(S.sones, 1)
+
+    eng = _engines(topo, core, [hc] + [cores[d] for d in direct[r]])
+    g.wait_ge(S.l1ml, 16)
+    g.remote_dma_fused([RemoteDMATransfer(
+        dst_ids=[_dst(topo, hc)] + [_dst(topo, cores[d]) for d in direct[r]],
+        dma_engine_mask=eng[0], remote_sem=S.mld, srcs=[T.mls[:, :]],
+        dsts=[T.mls[:, :]] + [T.mlg[_slot(direct, relay, d, r)] for d in direct[r]])], local_sem=S.sent)
+    g.wait_ge(S.l1o, 16)
+    g.remote_dma_fused([RemoteDMATransfer(
+        dst_ids=[_dst(topo, hc)], dma_engine_mask=eng[i], remote_sem=S.od,
+        src=T.opc[d], dst=T.opc[d]) for i, d in enumerate(relay[r])], local_sem=S.sent)
+    g.remote_dma_fused([RemoteDMATransfer(
+        dst_ids=[_dst(topo, cores[d])], dma_engine_mask=eng[i], remote_sem=S.od,
+        src=T.opc[d], dst=T.og[_slot(direct, relay, d, r)]) for i, d in enumerate(direct[r])], local_sem=S.sent)
+
+    g.wait_ge(S.sones, 1)
+    g.affine_select(T.P[0:16, :], T.ones[0:16, :], [[0, 8], [1, 16]], AluOpType.is_equal, 0.0, 0, -1).then_inc(S.sP, 1)
+    g.affine_select(T.mj0[:, :], T.ones[:, 0:8], [[-16, 8]], AluOpType.is_ge, 0.0, 0, 1).then_inc(S.smj0, 1)
+    g.wait_ge(S.smj0, 1)
+    g.affine_select(T.MJ[:, :], T.mj0[:, :], [[16, 8]], AluOpType.is_ge, 0.0, 15, -1).then_inc(S.sMJ, 1)
+    g.tensor.wait_ge(S.sP, 1)
+    g.tensor.matmul(T.PX[:, 0:128], T.P[0:16, :], T.P[0:16, :], True, True).then_inc(S.sPX, 1)
+    g.vector.wait_ge(S.sPX, 1)
+    g.vector.tensor_copy(T.X[:, :], T.PX[:, 0:128]).then_inc(S.sX, 1)
+
+    g.sync.wait_ge(S.mld, nd)
+    g.sync.dma_start(T.A[0:pd, :], T.mlg[0:nd, q0:q0 + 16, :]).then_inc(S.sA, 16)
+    g.scalar.wait_ge(S.od, nd)
+    g.scalar.dma_start(T.O[0:pd, 0:128], T.og[0:nd]).then_inc(S.sO, 16)
+    g.sync.wait_ge(S.mlr, nr)
+    g.sync.dma_start(T.A[pd:pr, :], T.mlg[nd:nd + nr, q0:q0 + 16, :]).then_inc(S.sA, 16)
+    g.sync.wait_ge(S.orl, nr)
+    g.sync.dma_start(T.O[pd:pr, 0:128], T.og[nd:nd + nr]).then_inc(S.sO, 16)
+
+    g.vector.wait_ge(S.sA, 48)
+    g.vector.wait_ge(S.sMJ, 1)
+    g.vector.tensor_scalar(T.Y[:, :], T.MJ[:, :], T.A[:, 0:1], None, mult).then_inc(S.sY, 1)
+    g.vector.tensor_copy(T.O[:, 128:129], T.A[:, 1:2]).then_inc(S.sL, 1)
+    g.tensor.wait_ge(S.sX, 1)
+    g.tensor.wait_ge(S.sY, 1)
+    g.tensor.matmul(T.PM[:, 0:8], T.X[:, :], T.Y[:, :], True, True).then_inc(S.sPM, 1)
+    g.vector.wait_ge(S.sPM, 1)
+    g.vector.tensor_reduce(T.negM[:, :], T.PM[:, 0:8], AxisListType.X, AluOpType.max, negate=True).then_inc(S.snegM, 1)
+    g.scalar.wait_ge(S.sA, 48)
+    g.scalar.wait_ge(S.snegM, 1)
+    g.scalar.activation(T.f[:, :], T.A[:, 0:1], Exp, bias=T.negM[:, 0:1]).then_inc(S.sf, 1)
+    g.vector.wait_ge(S.sX, 1)
+    g.vector.wait_ge(S.sf, 1)
+    g.vector.tensor_scalar(T.W[:, :], T.X[:, 0:16], T.f[:, 0:1], None, mult).then_inc(S.sW, 1)
+
+    g.tensor.wait_ge(S.sW, 1)
+    g.tensor.wait_ge(S.sL, 1)
+    g.tensor.wait_ge(S.sO, 48)
+    g.tensor.matmul(T.PO[0:16, 0:129], T.W[:, :], T.O[:, 0:129], True, True).then_inc(S.sPO, 1)
+    g.vector.wait_ge(S.sPO, 1)
+    g.vector.reciprocal(T.rec[0:16, :], T.PO[0:16, 128:129]).then_inc(S.srec, 1)
+    g.vector.wait_ge(S.srec, 1)
+    g.vector.tensor_scalar(T.yb[0:16, :], T.PO[0:16, 0:128], T.rec[0:16, 0:1], None, mult).then_inc(S.syb, 1)
+    g.sync.wait_ge(S.syb, 1)
+    g.sync.dma_start(T.y[:, :], T.yb[0:16, :]).then_inc(S.done, 16)
+    g.sync.wait_ge(S.done, 16)
+    g.wait_ge(S.sent, 1 + len(relay[r]) + len(direct[r]))

@@ -6,26 +6,31 @@ SCRATCH = {
     "mls": ("dram", [128, 2], "float32"),
     "og": ("dram", [7, 128, 16], "bfloat16"),
     "mlg": ("dram", [7, 128, 2], "float32"),
-    "O": ("sbuf", [128, 136], "bfloat16"),
+    "O": ("sbuf", [128, 128], "bfloat16"),
     "A": ("sbuf", [128, 2], "float32"),
-    "zz": ("sbuf", [128, 128], "bfloat16"),
+    "zz": ("sbuf", [128, 1], "float32"),
+    "one": ("sbuf", [128, 1], "float32"),
     "ones": ("sbuf", [128, 128], "bfloat16"),
-    "P": ("sbuf", [128, 128], "bfloat16"),
-    "X": ("sbuf", [128, 128], "bfloat16"),
     "mj0": ("sbuf", [128, 8], "bfloat16"),
+    "P": ("sbuf", [128, 128], "bfloat16"),
     "MJ": ("sbuf", [128, 8], "bfloat16"),
+    "X": ("sbuf", [128, 128], "bfloat16"),
+    "MN": ("sbuf", [128, 16], "float32"),
     "Y": ("sbuf", [128, 8], "bfloat16"),
+    "Ym": ("sbuf", [128, 16], "float32"),
+    "Lb": ("sbuf", [128, 1], "bfloat16"),
     "negM": ("sbuf", [128, 1], "float32"),
-    "f": ("sbuf", [128, 1], "float32"),
     "W": ("sbuf", [128, 16], "bfloat16"),
     "rec": ("sbuf", [128, 1], "float32"),
     "yb": ("sbuf", [128, 128], "bfloat16"),
     "PX": ("psum", [128, 512], "float32"),
     "PM": ("psum", [128, 512], "float32"),
-    "PO": ("psum", [128, 512], "float32"),
+    "PD": ("psum", [128, 512], "float32"),
+    "PO1": ("psum", [128, 512], "float32"),
+    "PO2": ("psum", [128, 512], "float32"),
 }
-SEMAPHORES = ["l1o", "l1ml", "sent", "mld", "od", "mlr", "orl", "sA", "sO", "sz", "sones", "sP", "sPX", "sX",
-              "smj0", "sMJ", "sY", "sL", "sPM", "snegM", "sf", "sW", "sPO", "srec", "syb", "done"]
+SEMAPHORES = ["l1o", "l1ml", "sent", "mld", "od", "mlr", "orl", "sA", "sO", "sz", "sone", "sel", "sP", "sPX", "sX",
+              "sMN", "sMJ", "sY", "sYm", "sL", "sPM", "snegM", "sW", "sPD", "srec", "sPO1", "sPO2", "syb", "done"]
 
 
 def _bits(mask):
@@ -35,7 +40,7 @@ def _bits(mask):
 def _plan(T, topo):
     cores = list(T.cores)
     n = len(cores)
-    direct, relay, helper = [], [], []
+    direct, relay, hml, ho = [], [], [], []
     for j in range(n):
         c = cores[j]
         direct.append([d for d in range(n) if d != j and topo.may_write(c, cores[d])])
@@ -43,9 +48,10 @@ def _plan(T, topo):
         cand = [h for h in range(128)
                 if topo.chip(h) == topo.chip(c) and h not in cores
                 and all(topo.may_write(h, cores[d]) for d in relay[j])]
-        near = [h for h in cand if topo.die(h) == topo.die(c)]
-        helper.append((near or cand)[0])
-    return cores, direct, relay, helper
+        cand = [h for h in cand if topo.die(h) == topo.die(c)] + [h for h in cand if topo.die(h) != topo.die(c)]
+        hml.append(cand[0])
+        ho.append(cand[1])
+    return cores, direct, relay, hml, ho
 
 
 def _slot(direct, relay, d, j):
@@ -67,27 +73,48 @@ def _engines(topo, src, dsts):
     return e[0::2] + e[1::2]
 
 
-def _helper_program(g, core, T, topo, j, cores, direct, relay):
+def _helper_program(g, core, T, topo, j, cores, direct, relay, for_ml):
     S = T.sem
     ds = relay[j]
-    eng = _engines(topo, core, [cores[d] for d in ds])
-    g.wait_ge(S.mld, 1)
-    g.remote_dma_fused([RemoteDMATransfer(
-        dst_ids=[_dst(topo, cores[d]) for d in ds], dma_engine_mask=eng[0], remote_sem=S.mlr,
-        srcs=[T.mls[:, :]], dsts=[T.mlg[_slot(direct, relay, d, j)] for d in ds])], local_sem=S.sent)
-    g.wait_ge(S.od, len(ds))
-    g.remote_dma_fused([RemoteDMATransfer(
-        dst_ids=[_dst(topo, cores[d])], dma_engine_mask=eng[i], remote_sem=S.orl,
-        src=T.opc[d], dst=T.og[_slot(direct, relay, d, j)]) for i, d in enumerate(ds)], local_sem=S.sent)
-    g.wait_ge(S.sent, 1 + len(ds))
+    eng = _engines(topo, core, [cores[j]] + [cores[d] for d in ds])
+    four = eng[0] | eng[1] | eng[2] | eng[3]
+    if for_ml:
+        g.vector.memset(T.ones[:, :], 1.0).then_inc(S.sz, 1)
+        g.wait_ge(S.sz, 1)
+        g.affine_select(T.P[:, :], T.ones[:, :], [[0, 8], [1, 16]], AluOpType.is_equal, 0.0, 0, -1).then_inc(S.sel, 1)
+        g.wait_ge(S.sel, 1)
+        g.remote_dma_fused([RemoteDMATransfer(
+            dst_ids=[_dst(topo, cores[j])], dma_engine_mask=four, remote_sem=S.sP,
+            src=T.P[:, :], dst=T.P[:, :])], local_sem=S.sent)
+        g.wait_ge(S.mld, 1)
+        g.remote_dma_fused([RemoteDMATransfer(
+            dst_ids=[_dst(topo, cores[d])], dma_engine_mask=eng[i], remote_sem=S.mlr,
+            src=T.mls[:, :], dst=T.mlg[_slot(direct, relay, d, j)]) for i, d in enumerate(ds)], local_sem=S.sent)
+    else:
+        g.vector.memset(T.ones[:, 0:8], 1.0).then_inc(S.sz, 1)
+        g.wait_ge(S.sz, 1)
+        g.affine_select(T.mj0[:, :], T.ones[:, 0:8], [[-16, 8]], AluOpType.is_ge, 0.0, 0, 1).then_inc(S.sel, 1)
+        g.wait_ge(S.sel, 1)
+        g.affine_select(T.MJ[:, :], T.mj0[:, :], [[16, 8]], AluOpType.is_ge, 0.0, 15, -1).then_inc(S.sel, 1)
+        g.wait_ge(S.sel, 2)
+        g.remote_dma_fused([RemoteDMATransfer(
+            dst_ids=[_dst(topo, cores[j])], dma_engine_mask=four, remote_sem=S.sMJ,
+            src=T.MJ[:, :], dst=T.MJ[:, :])], local_sem=S.sent)
+        g.wait_ge(S.od, len(ds))
+        g.remote_dma_fused([RemoteDMATransfer(
+            dst_ids=[_dst(topo, cores[d])], dma_engine_mask=eng[i], remote_sem=S.orl,
+            src=T.opc[d], dst=T.og[_slot(direct, relay, d, j)]) for i, d in enumerate(ds)], local_sem=S.sent)
+    g.wait_ge(S.sent, 4 + len(ds))
 
 
 def rank_program(g, core, T, topo):
-    cores, direct, relay, helper = _plan(T, topo)
+    cores, direct, relay, hml, ho = _plan(T, topo)
     r = T.rank_of(core)
     if r is None:
-        if core in helper:
-            _helper_program(g, core, T, topo, helper.index(core), cores, direct, relay)
+        if core in hml:
+            _helper_program(g, core, T, topo, hml.index(core), cores, direct, relay, True)
+        elif core in ho:
+            _helper_program(g, core, T, topo, ho.index(core), cores, direct, relay, False)
         return
     S = T.sem
     mult = AluOpType.mult
@@ -95,75 +122,78 @@ def rank_program(g, core, T, topo):
     nd = len([s for s in range(len(cores)) if r in direct[s]])
     nr = len([s for s in range(len(cores)) if r in relay[s]])
     q0, pd, pr = 16 * r, 16 * nd, 16 * (nd + nr)
-    hc = helper[r]
 
     g.sync.dma_start(T.opc[:], T.o[:, :]).then_inc(S.l1o, 16)
     g.scalar.dma_start(T.mls[:, :], T.ml[:, :]).then_inc(S.l1ml, 16)
-    g.sync.dma_start(T.O[pr:128, 0:128], T.o[q0:q0 + 16, :]).then_inc(S.sO, 16)
+    g.sync.dma_start(T.O[pr:128, :], T.o[q0:q0 + 16, :]).then_inc(S.sO, 16)
     g.scalar.dma_start(T.A[pr:128, :], T.ml[q0:q0 + 16, :]).then_inc(S.sA, 16)
 
     g.vector.memset(T.zz[:, :], 0.0).then_inc(S.sz, 1)
     g.scalar.wait_ge(S.sz, 1)
-    g.scalar.activation(T.ones[:, :], T.zz[:, :], Exp).then_inc(S.sones, 1)
+    g.scalar.activation(T.one[:, :], T.zz[:, :], Exp).then_inc(S.sone, 1)
 
-    eng = _engines(topo, core, [hc] + [cores[d] for d in direct[r]])
+    eng = _engines(topo, core, [hml[r], ho[r]] + [cores[d] for d in direct[r]])
     g.wait_ge(S.l1ml, 16)
     g.remote_dma_fused([RemoteDMATransfer(
-        dst_ids=[_dst(topo, hc)] + [_dst(topo, cores[d]) for d in direct[r]],
+        dst_ids=[_dst(topo, hml[r])] + [_dst(topo, cores[d]) for d in direct[r]],
         dma_engine_mask=eng[0], remote_sem=S.mld, srcs=[T.mls[:, :]],
         dsts=[T.mls[:, :]] + [T.mlg[_slot(direct, relay, d, r)] for d in direct[r]])], local_sem=S.sent)
     g.wait_ge(S.l1o, 16)
     g.remote_dma_fused([RemoteDMATransfer(
-        dst_ids=[_dst(topo, hc)], dma_engine_mask=eng[i], remote_sem=S.od,
+        dst_ids=[_dst(topo, ho[r])], dma_engine_mask=eng[i], remote_sem=S.od,
         src=T.opc[d], dst=T.opc[d]) for i, d in enumerate(relay[r])], local_sem=S.sent)
     g.remote_dma_fused([RemoteDMATransfer(
         dst_ids=[_dst(topo, cores[d])], dma_engine_mask=eng[i], remote_sem=S.od,
         src=T.opc[d], dst=T.og[_slot(direct, relay, d, r)]) for i, d in enumerate(direct[r])], local_sem=S.sent)
 
-    g.wait_ge(S.sones, 1)
-    g.affine_select(T.P[0:16, :], T.ones[0:16, :], [[0, 8], [1, 16]], AluOpType.is_equal, 0.0, 0, -1).then_inc(S.sP, 1)
-    g.affine_select(T.mj0[:, :], T.ones[:, 0:8], [[-16, 8]], AluOpType.is_ge, 0.0, 0, 1).then_inc(S.smj0, 1)
-    g.wait_ge(S.smj0, 1)
-    g.affine_select(T.MJ[:, :], T.mj0[:, :], [[16, 8]], AluOpType.is_ge, 0.0, 15, -1).then_inc(S.sMJ, 1)
-    g.tensor.wait_ge(S.sP, 1)
+    g.tensor.wait_ge(S.sP, 4)
     g.tensor.matmul(T.PX[:, 0:128], T.P[0:16, :], T.P[0:16, :], True, True).then_inc(S.sPX, 1)
     g.vector.wait_ge(S.sPX, 1)
     g.vector.tensor_copy(T.X[:, :], T.PX[:, 0:128]).then_inc(S.sX, 1)
+    g.vector.wait_ge(S.sone, 1)
+    g.vector.tensor_scalar(T.MN[:, :], T.PX[:, 0:16], T.one[:, 0:1], 1e20,
+                           AluOpType.subtract, mult).then_inc(S.sMN, 1)
 
     g.sync.wait_ge(S.mld, nd)
     g.sync.dma_start(T.A[0:pd, :], T.mlg[0:nd, q0:q0 + 16, :]).then_inc(S.sA, 16)
     g.scalar.wait_ge(S.od, nd)
-    g.scalar.dma_start(T.O[0:pd, 0:128], T.og[0:nd]).then_inc(S.sO, 16)
+    g.scalar.dma_start(T.O[0:pd, :], T.og[0:nd]).then_inc(S.sO, 16)
     g.sync.wait_ge(S.mlr, nr)
     g.sync.dma_start(T.A[pd:pr, :], T.mlg[nd:nd + nr, q0:q0 + 16, :]).then_inc(S.sA, 16)
     g.sync.wait_ge(S.orl, nr)
-    g.sync.dma_start(T.O[pd:pr, 0:128], T.og[nd:nd + nr]).then_inc(S.sO, 16)
+    g.sync.dma_start(T.O[pd:pr, :], T.og[nd:nd + nr]).then_inc(S.sO, 16)
 
     g.vector.wait_ge(S.sA, 48)
-    g.vector.wait_ge(S.sMJ, 1)
+    g.vector.wait_ge(S.sMJ, 4)
     g.vector.tensor_scalar(T.Y[:, :], T.MJ[:, :], T.A[:, 0:1], None, mult).then_inc(S.sY, 1)
-    g.vector.tensor_copy(T.O[:, 128:129], T.A[:, 1:2]).then_inc(S.sL, 1)
+    g.vector.wait_ge(S.sMN, 1)
+    g.vector.tensor_scalar(T.Ym[:, :], T.MN[:, :], T.A[:, 0:1], None, AluOpType.add).then_inc(S.sYm, 1)
+    g.vector.tensor_copy(T.Lb[:, :], T.A[:, 1:2]).then_inc(S.sL, 1)
     g.tensor.wait_ge(S.sX, 1)
     g.tensor.wait_ge(S.sY, 1)
     g.tensor.matmul(T.PM[:, 0:8], T.X[:, :], T.Y[:, :], True, True).then_inc(S.sPM, 1)
     g.vector.wait_ge(S.sPM, 1)
     g.vector.tensor_reduce(T.negM[:, :], T.PM[:, 0:8], AxisListType.X, AluOpType.max, negate=True).then_inc(S.snegM, 1)
-    g.scalar.wait_ge(S.sA, 48)
+    g.scalar.wait_ge(S.sYm, 1)
     g.scalar.wait_ge(S.snegM, 1)
-    g.scalar.activation(T.f[:, :], T.A[:, 0:1], Exp, bias=T.negM[:, 0:1]).then_inc(S.sf, 1)
-    g.vector.wait_ge(S.sX, 1)
-    g.vector.wait_ge(S.sf, 1)
-    g.vector.tensor_scalar(T.W[:, :], T.X[:, 0:16], T.f[:, 0:1], None, mult).then_inc(S.sW, 1)
-
+    g.scalar.activation(T.W[:, :], T.Ym[:, :], Exp, bias=T.negM[:, 0:1]).then_inc(S.sW, 1)
     g.tensor.wait_ge(S.sW, 1)
     g.tensor.wait_ge(S.sL, 1)
+    g.tensor.matmul(T.PD[0:16, 0:1], T.W[:, :], T.Lb[:, :], True, True).then_inc(S.sPD, 1)
+    g.vector.wait_ge(S.sPD, 1)
+    g.vector.reciprocal(T.rec[0:16, :], T.PD[0:16, 0:1]).then_inc(S.srec, 1)
+
     g.tensor.wait_ge(S.sO, 48)
-    g.tensor.matmul(T.PO[0:16, 0:129], T.W[:, :], T.O[:, 0:129], True, True).then_inc(S.sPO, 1)
-    g.vector.wait_ge(S.sPO, 1)
-    g.vector.reciprocal(T.rec[0:16, :], T.PO[0:16, 128:129]).then_inc(S.srec, 1)
+    g.tensor.matmul(T.PO1[0:16, 0:64], T.W[:, :], T.O[:, 0:64], True, True).then_inc(S.sPO1, 1)
+    g.tensor.matmul(T.PO2[0:16, 0:64], T.W[:, :], T.O[:, 64:128], True, True).then_inc(S.sPO2, 1)
     g.vector.wait_ge(S.srec, 1)
-    g.vector.tensor_scalar(T.yb[0:16, :], T.PO[0:16, 0:128], T.rec[0:16, 0:1], None, mult).then_inc(S.syb, 1)
-    g.sync.wait_ge(S.syb, 1)
+    g.vector.wait_ge(S.sPO1, 1)
+    g.vector.tensor_scalar(T.yb[0:16, 0:64], T.PO1[0:16, 0:64], T.rec[0:16, 0:1], None, mult).then_inc(S.syb, 1)
+    g.scalar.wait_ge(S.srec, 1)
+    g.scalar.wait_ge(S.sPO2, 1)
+    g.scalar.activation(T.yb[0:16, 64:128], T.PO2[0:16, 0:64], ActivationFunctionType.Copy,
+                        scale=T.rec[0:16, 0:1]).then_inc(S.syb, 1)
+    g.sync.wait_ge(S.syb, 2)
     g.sync.dma_start(T.y[:, :], T.yb[0:16, :]).then_inc(S.done, 16)
     g.sync.wait_ge(S.done, 16)
     g.wait_ge(S.sent, 1 + len(relay[r]) + len(direct[r]))

@@ -11,8 +11,11 @@ SCRATCH = {
     "zz": ("sbuf", [128, 1], "float32"),
     "one": ("sbuf", [128, 1], "float32"),
     "ones": ("sbuf", [128, 128], "bfloat16"),
-    "mj0": ("sbuf", [128, 8], "bfloat16"),
+    "Ph": ("sbuf", [128, 64], "bfloat16"),
     "P": ("sbuf", [128, 128], "bfloat16"),
+    "V0": ("sbuf", [128, 8], "bfloat16"),
+    "V": ("sbuf", [128, 8], "bfloat16"),
+    "Vc": ("sbuf", [128, 8], "bfloat16"),
     "MJ": ("sbuf", [128, 8], "bfloat16"),
     "X": ("sbuf", [128, 128], "bfloat16"),
     "MN": ("sbuf", [128, 16], "float32"),
@@ -30,7 +33,8 @@ SCRATCH = {
     "PO2": ("psum", [128, 512], "float32"),
 }
 SEMAPHORES = ["l1o", "l1ml", "sent", "mld", "od", "mlr", "orl", "sA", "sO", "sz", "sone", "sel", "sP", "sPX", "sX",
-              "sMN", "sMJ", "sY", "sYm", "sL", "sPM", "snegM", "sW", "sPD", "srec", "sPO1", "sPO2", "syb", "done"]
+              "sMN", "sV", "sVc", "sMJ", "sY", "sYm", "sL", "sPM", "snegM", "sW", "sPD", "srec", "sPO1", "sPO2",
+              "syb", "done"]
 
 
 def _bits(mask):
@@ -77,34 +81,27 @@ def _helper_program(g, core, T, topo, j, cores, direct, relay, for_ml):
     S = T.sem
     ds = relay[j]
     eng = _engines(topo, core, [cores[j]] + [cores[d] for d in ds])
-    four = eng[0] | eng[1] | eng[2] | eng[3]
+    every = 0
+    for e in eng:
+        every |= e
+    g.vector.memset(T.ones[:, 0:64], 1.0).then_inc(S.sz, 1)
+    g.wait_ge(S.sz, 1)
+    g.affine_select(T.Ph[:, :], T.ones[:, 0:64], [[0, 4], [1, 16]], AluOpType.is_equal, 0.0, 0, -1).then_inc(S.sel, 1)
+    g.wait_ge(S.sel, 1)
+    g.remote_dma_fused([RemoteDMATransfer(
+        dst_ids=[_dst(topo, cores[j])], dma_engine_mask=every, remote_sem=S.sP,
+        src=T.Ph[:, :], dst=T.P[:, 0:64] if for_ml else T.P[:, 64:128])], local_sem=S.sent)
     if for_ml:
-        g.vector.memset(T.ones[:, :], 1.0).then_inc(S.sz, 1)
-        g.wait_ge(S.sz, 1)
-        g.affine_select(T.P[:, :], T.ones[:, :], [[0, 8], [1, 16]], AluOpType.is_equal, 0.0, 0, -1).then_inc(S.sel, 1)
-        g.wait_ge(S.sel, 1)
-        g.remote_dma_fused([RemoteDMATransfer(
-            dst_ids=[_dst(topo, cores[j])], dma_engine_mask=four, remote_sem=S.sP,
-            src=T.P[:, :], dst=T.P[:, :])], local_sem=S.sent)
         g.wait_ge(S.mld, 1)
         g.remote_dma_fused([RemoteDMATransfer(
             dst_ids=[_dst(topo, cores[d])], dma_engine_mask=eng[i], remote_sem=S.mlr,
             src=T.mls[:, :], dst=T.mlg[_slot(direct, relay, d, j)]) for i, d in enumerate(ds)], local_sem=S.sent)
     else:
-        g.vector.memset(T.ones[:, 0:8], 1.0).then_inc(S.sz, 1)
-        g.wait_ge(S.sz, 1)
-        g.affine_select(T.mj0[:, :], T.ones[:, 0:8], [[-16, 8]], AluOpType.is_ge, 0.0, 0, 1).then_inc(S.sel, 1)
-        g.wait_ge(S.sel, 1)
-        g.affine_select(T.MJ[:, :], T.mj0[:, :], [[16, 8]], AluOpType.is_ge, 0.0, 15, -1).then_inc(S.sel, 1)
-        g.wait_ge(S.sel, 2)
-        g.remote_dma_fused([RemoteDMATransfer(
-            dst_ids=[_dst(topo, cores[j])], dma_engine_mask=four, remote_sem=S.sMJ,
-            src=T.MJ[:, :], dst=T.MJ[:, :])], local_sem=S.sent)
         g.wait_ge(S.od, len(ds))
         g.remote_dma_fused([RemoteDMATransfer(
             dst_ids=[_dst(topo, cores[d])], dma_engine_mask=eng[i], remote_sem=S.orl,
             src=T.opc[d], dst=T.og[_slot(direct, relay, d, j)]) for i, d in enumerate(ds)], local_sem=S.sent)
-    g.wait_ge(S.sent, 4 + len(ds))
+    g.wait_ge(S.sent, len(eng) + len(ds))
 
 
 def rank_program(g, core, T, topo):
@@ -119,8 +116,9 @@ def rank_program(g, core, T, topo):
     S = T.sem
     mult = AluOpType.mult
     Exp = ActivationFunctionType.Exp
-    nd = len([s for s in range(len(cores)) if r in direct[s]])
-    nr = len([s for s in range(len(cores)) if r in relay[s]])
+    n = len(cores)
+    nd = len([s for s in range(n) if r in direct[s]])
+    nr = len([s for s in range(n) if r in relay[s]])
     q0, pd, pr = 16 * r, 16 * nd, 16 * (nd + nr)
 
     g.sync.dma_start(T.opc[:], T.o[:, :]).then_inc(S.l1o, 16)
@@ -133,6 +131,15 @@ def rank_program(g, core, T, topo):
     g.scalar.activation(T.one[:, :], T.zz[:, :], Exp).then_inc(S.sone, 1)
 
     eng = _engines(topo, core, [hml[r], ho[r]] + [cores[d] for d in direct[r]])
+    apart = eng[4] | eng[5] | eng[6] | eng[7]
+    nxt = [[(s + k) % n for k in range(1, n) if (s + k) % n in direct[s]][0] for s in range(n)]
+    nv = len([s for s in range(n) if nxt[s] == r])
+    g.iota(T.V0[:, :], [[-16, 8]], 0, 1, allow_small_or_imprecise_dtypes=True).then_inc(S.sel, 1)
+    g.wait_ge(S.sel, 1)
+    g.remote_dma_fused([RemoteDMATransfer(
+        dst_ids=[_dst(topo, cores[nxt[r]])], dma_engine_mask=apart, remote_sem=S.sV,
+        src=T.V0[:, :], dst=T.V[:, :])], local_sem=S.sent)
+
     g.wait_ge(S.l1ml, 16)
     g.remote_dma_fused([RemoteDMATransfer(
         dst_ids=[_dst(topo, hml[r])] + [_dst(topo, cores[d]) for d in direct[r]],
@@ -146,13 +153,19 @@ def rank_program(g, core, T, topo):
         dst_ids=[_dst(topo, cores[d])], dma_engine_mask=eng[i], remote_sem=S.od,
         src=T.opc[d], dst=T.og[_slot(direct, relay, d, r)]) for i, d in enumerate(direct[r])], local_sem=S.sent)
 
-    g.tensor.wait_ge(S.sP, 4)
+    nP = len(_engines(topo, hml[r], [core] + [cores[d] for d in relay[r]])) \
+        + len(_engines(topo, ho[r], [core] + [cores[d] for d in relay[r]]))
+    g.tensor.wait_ge(S.sP, nP)
     g.tensor.matmul(T.PX[:, 0:128], T.P[0:16, :], T.P[0:16, :], True, True).then_inc(S.sPX, 1)
     g.vector.wait_ge(S.sPX, 1)
     g.vector.tensor_copy(T.X[:, :], T.PX[:, 0:128]).then_inc(S.sX, 1)
     g.vector.wait_ge(S.sone, 1)
     g.vector.tensor_scalar(T.MN[:, :], T.PX[:, 0:16], T.one[:, 0:1], 1e20,
                            AluOpType.subtract, mult).then_inc(S.sMN, 1)
+    g.vector.wait_ge(S.sV, 4 * nv)
+    g.vector.tensor_scalar(T.Vc[:, :], T.V[:, :], 0.0, 15.0, AluOpType.max, AluOpType.min).then_inc(S.sVc, 1)
+    g.vector.wait_ge(S.sVc, 1)
+    g.vector.tensor_tensor(T.MJ[:, :], T.Vc[:, :], T.V[:, :], AluOpType.is_equal).then_inc(S.sMJ, 1)
 
     g.sync.wait_ge(S.mld, nd)
     g.sync.dma_start(T.A[0:pd, :], T.mlg[0:nd, q0:q0 + 16, :]).then_inc(S.sA, 16)
@@ -164,7 +177,7 @@ def rank_program(g, core, T, topo):
     g.sync.dma_start(T.O[pd:pr, :], T.og[nd:nd + nr]).then_inc(S.sO, 16)
 
     g.vector.wait_ge(S.sA, 48)
-    g.vector.wait_ge(S.sMJ, 4)
+    g.vector.wait_ge(S.sMJ, 1)
     g.vector.tensor_scalar(T.Y[:, :], T.MJ[:, :], T.A[:, 0:1], None, mult).then_inc(S.sY, 1)
     g.vector.wait_ge(S.sMN, 1)
     g.vector.tensor_scalar(T.Ym[:, :], T.MN[:, :], T.A[:, 0:1], None, AluOpType.add).then_inc(S.sYm, 1)
@@ -196,4 +209,4 @@ def rank_program(g, core, T, topo):
     g.sync.wait_ge(S.syb, 2)
     g.sync.dma_start(T.y[:, :], T.yb[0:16, :]).then_inc(S.done, 16)
     g.sync.wait_ge(S.done, 16)
-    g.wait_ge(S.sent, 1 + len(relay[r]) + len(direct[r]))
+    g.wait_ge(S.sent, 4 + 1 + len(relay[r]) + len(direct[r]))

from concourse.bass import DstId, RemoteDMATransfer
from concourse.mybir import AluOpType, AxisListType, ActivationFunctionType

SCRATCH = {
    "opc": ("dram", [8, 128, 16], "bfloat16"),
    "mls": ("dram", [128, 2], "float32"),
    "og": ("dram", [7, 128, 16], "bfloat16"),
    "mlg": ("dram", [7, 128, 2], "float32"),
    "O": ("sbuf", [128, 128], "bfloat16"),
    "A": ("sbuf", [128, 2], "float32"),
    "zz": ("sbuf", [128, 1], "float32"),
    "one": ("sbuf", [128, 1], "float32"),
    "ones": ("sbuf", [128, 128], "bfloat16"),
    "Ph": ("sbuf", [128, 64], "bfloat16"),
    "P": ("sbuf", [128, 128], "bfloat16"),
    "V0": ("sbuf", [128, 8], "bfloat16"),
    "V": ("sbuf", [128, 8], "bfloat16"),
    "Vc": ("sbuf", [128, 8], "bfloat16"),
    "MJ": ("sbuf", [128, 8], "bfloat16"),
    "X": ("sbuf", [128, 128], "bfloat16"),
    "MN": ("sbuf", [128, 16], "float32"),
    "Y": ("sbuf", [128, 8], "bfloat16"),
    "Ym": ("sbuf", [128, 16], "float32"),
    "Lb": ("sbuf", [128, 1], "bfloat16"),
    "negM": ("sbuf", [128, 1], "float32"),
    "W": ("sbuf", [128, 16], "bfloat16"),
    "rec": ("sbuf", [128, 1], "float32"),
    "yb": ("sbuf", [128, 128], "bfloat16"),
    "PX": ("psum", [128, 512], "float32"),
    "PM": ("psum", [128, 512], "float32"),
    "PD": ("psum", [128, 512], "float32"),
    "PO1": ("psum", [128, 512], "float32"),
    "PO2": ("psum", [128, 512], "float32"),
}
SEMAPHORES = ["l1o", "l1ml", "sent", "mld", "od", "mlr", "orl", "sA", "sO", "sz", "sone", "sel", "sP", "sPX", "sX",
              "sMN", "sV", "sVc", "sMJ", "sY", "sYm", "sL", "sPM", "snegM", "sW", "sPD", "srec", "sPO1", "sPO2",
              "syb", "done"]


def _bits(mask):
    return [1 << i for i in range(16) if (mask >> i) & 1]


def _plan(T, topo):
    cores = list(T.cores)
    n = len(cores)
    direct, relay, hml, ho = [], [], [], []
    for j in range(n):
        c = cores[j]
        direct.append([d for d in range(n) if d != j and topo.may_write(c, cores[d])])
        relay.append([d for d in range(n) if d != j and not topo.may_write(c, cores[d])])
        cand = [h for h in range(128)
                if topo.chip(h) == topo.chip(c) and h not in cores
                and all(topo.may_write(h, cores[d]) for d in relay[j])]
        cand = [h for h in cand if topo.die(h) == topo.die(c)] + [h for h in cand if topo.die(h) != topo.die(c)]
        hml.append(cand[0])
        ho.append(cand[1])
    return cores, direct, relay, hml, ho


def _slot(direct, relay, d, j):
    n = len(direct)
    order = [s for s in range(n) if d in direct[s]] + [s for s in range(n) if d in relay[s]]
    return order.index(j)


def _dst(topo, c):
    rid, pid, _ = topo.addr(c)
    return DstId(rid=rid, pnc=pid)


def _engines(topo, src, dsts):
    m = topo.mask(src, dsts[0])
    for d in dsts[1:]:
        m &= topo.mask(src, d)
    e = _bits(m)
    return e[0::2] + e[1::2]


def _helper_program(g, core, T, topo, j, cores, direct, relay, for_ml):
    S = T.sem
    ds = relay[j]
    eng = _engines(topo, core, [cores[j]] + [cores[d] for d in ds])
    every = 0
    for e in eng:
        every |= e
    g.vector.memset(T.ones[:, 0:64], 1.0).then_inc(S.sz, 1)
    g.wait_ge(S.sz, 1)
    g.affine_select(T.Ph[:, :], T.ones[:, 0:64], [[0, 4], [1, 16]], AluOpType.is_equal, 0.0, 0, -1).then_inc(S.sel, 1)
    g.wait_ge(S.sel, 1)
    g.remote_dma_fused([RemoteDMATransfer(
        dst_ids=[_dst(topo, cores[j])], dma_engine_mask=every, remote_sem=S.sP,
        src=T.Ph[:, :], dst=T.P[:, 0:64] if for_ml else T.P[:, 64:128])], local_sem=S.sent)
    if for_ml:
        g.wait_ge(S.mld, 1)
        g.remote_dma_fused([RemoteDMATransfer(
            dst_ids=[_dst(topo, cores[d])], dma_engine_mask=eng[i], remote_sem=S.mlr,
            src=T.mls[:, :], dst=T.mlg[_slot(direct, relay, d, j)]) for i, d in enumerate(ds)], local_sem=S.sent)
    else:
        g.wait_ge(S.od, len(ds))
        g.remote_dma_fused([RemoteDMATransfer(
            dst_ids=[_dst(topo, cores[d])], dma_engine_mask=eng[i], remote_sem=S.orl,
            src=T.opc[d], dst=T.og[_slot(direct, relay, d, j)]) for i, d in enumerate(ds)], local_sem=S.sent)
    g.wait_ge(S.sent, len(eng) + len(ds))


def rank_program(g, core, T, topo):
    cores, direct, relay, hml, ho = _plan(T, topo)
    r = T.rank_of(core)
    if r is None:
        if core in hml:
            _helper_program(g, core, T, topo, hml.index(core), cores, direct, relay, True)
        elif core in ho:
            _helper_program(g, core, T, topo, ho.index(core), cores, direct, relay, False)
        return
    S = T.sem
    mult = AluOpType.mult
    Exp = ActivationFunctionType.Exp
    n = len(cores)
    nd = len([s for s in range(n) if r in direct[s]])
    nr = len([s for s in range(n) if r in relay[s]])
    q0, pd, pr = 16 * r, 16 * nd, 16 * (nd + nr)

    g.sync.dma_start(T.opc[:], T.o[:, :]).then_inc(S.l1o, 16)
    g.scalar.dma_start(T.mls[:, :], T.ml[:, :]).then_inc(S.l1ml, 16)
    g.sync.dma_start(T.O[pr:128, :], T.o[q0:q0 + 16, :]).then_inc(S.sO, 16)
    g.scalar.dma_start(T.A[pr:128, :], T.ml[q0:q0 + 16, :]).then_inc(S.sA, 16)

    g.vector.memset(T.zz[:, :], 0.0).then_inc(S.sz, 1)
    g.scalar.wait_ge(S.sz, 1)
    g.scalar.activation(T.one[:, :], T.zz[:, :], Exp).then_inc(S.sone, 1)

    eng = _engines(topo, core, [hml[r], ho[r]] + [cores[d] for d in direct[r]])
    apart = eng[4] | eng[5] | eng[6] | eng[7]
    nxt = [[(s + k) % n for k in range(1, n) if (s + k) % n in direct[s]][0] for s in range(n)]
    nv = len([s for s in range(n) if nxt[s] == r])
    g.iota(T.V0[:, :], [[-16, 8]], 0, 1, allow_small_or_imprecise_dtypes=True).then_inc(S.sel, 1)
    g.wait_ge(S.sel, 1)
    g.remote_dma_fused([RemoteDMATransfer(
        dst_ids=[_dst(topo, cores[nxt[r]])], dma_engine_mask=apart, remote_sem=S.sV,
        src=T.V0[:, :], dst=T.V[:, :])], local_sem=S.sent)

    g.wait_ge(S.l1ml, 16)
    g.remote_dma_fused([RemoteDMATransfer(
        dst_ids=[_dst(topo, hml[r])] + [_dst(topo, cores[d]) for d in direct[r]],
        dma_engine_mask=eng[0], remote_sem=S.mld, srcs=[T.mls[:, :]],
        dsts=[T.mls[:, :]] + [T.mlg[_slot(direct, relay, d, r)] for d in direct[r]])], local_sem=S.sent)
    g.wait_ge(S.l1o, 16)
    g.remote_dma_fused([RemoteDMATransfer(
        dst_ids=[_dst(topo, ho[r])], dma_engine_mask=eng[i], remote_sem=S.od,
        src=T.opc[d], dst=T.opc[d]) for i, d in enumerate(relay[r])], local_sem=S.sent)
    g.remote_dma_fused([RemoteDMATransfer(
        dst_ids=[_dst(topo, cores[d])], dma_engine_mask=eng[i], remote_sem=S.od,
        src=T.opc[d], dst=T.og[_slot(direct, relay, d, r)]) for i, d in enumerate(direct[r])], local_sem=S.sent)

    nP = len(_engines(topo, hml[r], [core] + [cores[d] for d in relay[r]])) \
        + len(_engines(topo, ho[r], [core] + [cores[d] for d in relay[r]]))
    g.tensor.wait_ge(S.sP, nP)
    g.tensor.matmul(T.PX[:, 0:128], T.P[0:16, :], T.P[0:16, :], True, True).then_inc(S.sPX, 1)
    g.vector.wait_ge(S.sPX, 1)
    g.vector.tensor_copy(T.X[:, :], T.PX[:, 0:128]).then_inc(S.sX, 1)
    g.vector.wait_ge(S.sone, 1)
    g.vector.tensor_scalar(T.MN[:, :], T.PX[:, 0:16], T.one[:, 0:1], 1e20,
                           AluOpType.subtract, mult).then_inc(S.sMN, 1)
    g.vector.wait_ge(S.sV, 4 * nv)
    g.vector.tensor_scalar(T.Vc[:, :], T.V[:, :], 0.0, 15.0, AluOpType.max, AluOpType.min).then_inc(S.sVc, 1)
    g.vector.wait_ge(S.sVc, 1)
    g.vector.tensor_tensor(T.MJ[:, :], T.Vc[:, :], T.V[:, :], AluOpType.is_equal).then_inc(S.sMJ, 1)

    g.sync.wait_ge(S.mld, nd)
    g.sync.dma_start(T.A[0:pd, :], T.mlg[0:nd, q0:q0 + 16, :]).then_inc(S.sA, 16)
    g.scalar.wait_ge(S.od, nd)
    g.scalar.dma_start(T.O[0:pd, :], T.og[0:nd]).then_inc(S.sO, 16)
    g.sync.wait_ge(S.mlr, nr)
    g.sync.dma_start(T.A[pd:pr, :], T.mlg[nd:nd + nr, q0:q0 + 16, :]).then_inc(S.sA, 16)
    g.sync.wait_ge(S.orl, nr)
    g.sync.dma_start(T.O[pd:pr, :], T.og[nd:nd + nr]).then_inc(S.sO, 16)

    g.vector.wait_ge(S.sA, 48)
    g.vector.wait_ge(S.sMJ, 1)
    g.vector.tensor_scalar(T.Y[:, :], T.MJ[:, :], T.A[:, 0:1], None, mult).then_inc(S.sY, 1)
    g.vector.wait_ge(S.sMN, 1)
    g.vector.tensor_scalar(T.Ym[:, :], T.MN[:, :], T.A[:, 0:1], None, AluOpType.add).then_inc(S.sYm, 1)
    g.vector.tensor_copy(T.Lb[:, :], T.A[:, 1:2]).then_inc(S.sL, 1)
    g.tensor.wait_ge(S.sX, 1)
    g.tensor.wait_ge(S.sY, 1)
    g.tensor.matmul(T.PM[:, 0:8], T.X[:, :], T.Y[:, :], True, True).then_inc(S.sPM, 1)
    g.vector.wait_ge(S.sPM, 1)
    g.vector.tensor_reduce(T.negM[:, :], T.PM[:, 0:8], AxisListType.X, AluOpType.max, negate=True).then_inc(S.snegM, 1)
    g.scalar.wait_ge(S.sYm, 1)
    g.scalar.wait_ge(S.snegM, 1)
    g.scalar.activation(T.W[:, :], T.Ym[:, :], Exp, bias=T.negM[:, 0:1]).then_inc(S.sW, 1)
    g.tensor.wait_ge(S.sW, 1)
    g.tensor.wait_ge(S.sL, 1)
    g.tensor.matmul(T.PD[0:16, 0:1], T.W[:, :], T.Lb[:, :], True, True).then_inc(S.sPD, 1)
    g.vector.wait_ge(S.sPD, 1)
    g.vector.reciprocal(T.rec[0:16, :], T.PD[0:16, 0:1]).then_inc(S.srec, 1)

    g.tensor.wait_ge(S.sO, 48)
    g.tensor.matmul(T.PO1[0:16, 0:64], T.W[:, :], T.O[:, 0:64], True, True).then_inc(S.sPO1, 1)
    g.tensor.matmul(T.PO2[0:16, 0:64], T.W[:, :], T.O[:, 64:128], True, True).then_inc(S.sPO2, 1)
    g.vector.wait_ge(S.srec, 1)
    g.vector.wait_ge(S.sPO1, 1)
    g.vector.tensor_scalar(T.yb[0:16, 0:64], T.PO1[0:16, 0:64], T.rec[0:16, 0:1], None, mult).then_inc(S.syb, 1)
    g.scalar.wait_ge(S.srec, 1)
    g.scalar.wait_ge(S.sPO2, 1)
    g.scalar.activation(T.yb[0:16, 64:128], T.PO2[0:16, 0:64], ActivationFunctionType.Copy,
                        scale=T.rec[0:16, 0:1]).then_inc(S.syb, 1)
    g.sync.wait_ge(S.syb, 2)
    g.sync.dma_start(T.y[:, :], T.yb[0:16, :]).then_inc(S.done, 16)
    g.sync.wait_ge(S.done, 16)
    g.wait_ge(S.sent, 4 + 1 + len(relay[r]) + len(direct[r]))
